import numpy as np
import ml_dtypes


def mxq(x, axis, fmt="e4m3"):
    dtype, down = {"e4m3": (ml_dtypes.float8_e4m3fn, 7), "e5m2": (ml_dtypes.float8_e5m2, 14)}[fmt]
    v = np.moveaxis(np.asarray(x, np.float32).astype(ml_dtypes.bfloat16).astype(np.float64), axis, -1)
    blocks = v.reshape(v.shape[:-1] + (-1, 32))
    amax = np.abs(blocks).max(-1, keepdims=True)
    byte = np.maximum(np.where(amax > 0, np.frexp(amax)[1] - 1 + 127, 0) - down, 1)
    scale = np.exp2(byte - 127.0)
    codes = (blocks / scale).astype(np.float32).astype(dtype).astype(np.float64)
    return np.moveaxis((codes * scale).reshape(v.shape), -1, axis)


WIDE = False


def mx_kscale(k):
    if not WIDE:
        return np.ones(k)
    levels = np.array([30, -30])
    if k % 512:
        return np.exp2(np.random.permutation(np.resize(levels, k // 32))).repeat(32)
    a = np.empty((k // 512, 16))
    for p in range(k // 512):
        a[p, :8] = np.random.permutation(np.resize(levels, 8))
        for g in range(8):
            far = levels[np.abs(levels - a[p, g]) >= 10]
            a[p, g + 8] = far[np.random.randint(len(far))]
    return np.exp2(a.ravel()).repeat(32)


BF16 = ml_dtypes.bfloat16


def bf(x):
    return np.asarray(x, np.float32).astype(BF16)


def f64(x):
    return np.asarray(x).astype(np.float64)


T, D, F, G = 512, 1024, 1536, 2048


def setup_inputs():
    s = mx_kscale(D)
    t1 = mx_kscale(F)
    t2 = mx_kscale(G)
    n = np.random.standard_normal
    return {
        "dy": bf(n((T, D)) * np.exp(0.5 * n((T, D))) * s),
        "dec1": bf(n((F, D)) / np.sqrt(D) / s * t1[:, None]),
        "dec2": bf(n((G, D)) / np.sqrt(D) / s * t2[:, None]),
        "pen1": bf(0.3 * np.abs(n(F)) * t1),
        "pen2": bf(0.3 * np.abs(n(G)) * t2),
        "gate1": bf(np.random.random((T, F)) < 0.5),
        "gate2": bf(np.random.random((T, G)) < 0.5),
        "enc1": bf(n((D, F)) / np.sqrt(F) / t1),
        "enc2": bf(n((D, G)) / np.sqrt(G) / t2),
    }


def reference(dy, dec1, dec2, pen1, pen2, gate1, gate2, enc1, enc2):
    qy = mxq(f64(dy), 1, "e5m2")
    df1 = ((qy @ mxq(f64(dec1), 1, "e4m3").T) + f64(pen1)) * f64(gate1)
    df2 = ((qy @ mxq(f64(dec2), 1, "e4m3").T) + f64(pen2)) * f64(gate2)
    dx2 = mxq(df2, 1, "e5m2") @ mxq(f64(enc2), 1, "e4m3").T
    dx1 = mxq(df1, 1, "e5m2") @ mxq(f64(enc1), 1, "e4m3").T
    return dx1 + dx2, dx2

@@ -1,0 +1,267 @@
+from contextlib import ExitStack
+
+import concourse.mybir as mybir
+from concourse.masks import make_identity
+
+T, D, F, G = 512, 1024, 1536, 2048
+FLOPS = 4 * T * D * (F + G)
+
+F32 = mybir.dt.float32
+BF16 = mybir.dt.bfloat16
+U32 = mybir.dt.uint32
+U8 = mybir.dt.uint8
+E4M3 = mybir.dt.float8_e4m3fn_x4
+E5M2 = mybir.dt.float8_e5m2_x4
+IDENTITY = mybir.ActivationFunctionType.Identity
+ALU = mybir.AluOpType
+
+P = 128
+K_PASS = 512
+WORDS = K_PASS // 2
+COLS = 2 * P
+N = 512
+LATE_GROUPS = G // K_PASS
+GROUPS = (F + G) // K_PASS
+UNITS = 2 * GROUPS
+
+ENC_PER_STEP = [0, 0] + [1] * 8 + [2] * 4 + [2, 4, 3, 3, 0]
+DX_PER_STEP = [0] * 10 + [1] * 4 + [2, 2, 2, 2, 4]
+GATE_LAG = 2
+LOAD_AHEAD = 3
+SORT_AHEAD = 4
+Q_LAG = 2
+Q_LAG_GATE = 2
+DEC_BUFS, GATE_BUFS, ENC_BUFS, SORT_BUFS, GROUP_BUFS, ACC_BUFS = 5, 6, 6, 6, 5, 2
+
+
+def ORDER(decs, gates, encs):
+    return decs + gates + encs
+
+
+def SORT(s, b):
+    return "v" if b[0] == "enc" else ""
+
+
+def EMPTY(s, b):
+    return "s"
+
+
+def tile_cross_layer_transcoder_backward_s6_kernel(
+    tc, dy, dec1, dec2, pen1, pen2, gate1, gate2, enc1, enc2, out_0, out_1
+):
+    nc = tc.nc
+
+    def layer(g):
+        if g < LATE_GROUPS:
+            return dec2, gate2, enc2, g
+        return dec1, gate1, enc1, g - LATE_GROUPS
+
+    late = list(range(LATE_GROUPS))
+    early = list(range(LATE_GROUPS, GROUPS))
+    enc_blocks = [("enc", h, g, pair) for gs in (late, early) for h in range(2) for pair in range(2) for g in gs]
+    dx_tiles = [("dx", h, j, gs) for gs in (late, early) for h in range(2) for j in range(T // P)]
+    steps = [([("dy", jj, c) for jj in range(2) for c in range(2)] + [("dec", 0, c) for c in range(2)], [])]
+    ne, nd = 0, 0
+    for i in range(len(ENC_PER_STEP)):
+        blocks, mms = [], []
+        decs = [("dec", i + 1, c) for c in range(2)] if i + 1 < UNITS else []
+        gates = [("gate", u // 2, u % 2) for u in range(UNITS) if min(u + GATE_LAG, UNITS) == i]
+        encs = enc_blocks[ne : ne + ENC_PER_STEP[i]]
+        ne = ne + ENC_PER_STEP[i]
+        blocks = ORDER(decs, gates, encs)
+        if i < UNITS:
+            mms = [("df", i, a) for a in range(2)]
+        mms = mms + dx_tiles[nd : nd + DX_PER_STEP[i]]
+        nd = nd + DX_PER_STEP[i]
+        steps.append((blocks, mms))
+    assert ne == len(enc_blocks) and nd == len(dx_tiles)
+
+    with ExitStack() as ctx:
+        keep = ctx.enter_context(tc.tile_pool(name="keep", bufs=1))
+        raw_pool = ctx.enter_context(tc.tile_pool(name="raw", bufs=1))
+        work = ctx.enter_context(tc.tile_pool(name="work", bufs=1))
+        psum = ctx.enter_context(tc.psum_pool(name="psum", bufs=8))
+        ctx.enter_context(tc.manual_schedule())
+
+        ident = keep.tile([P, P], F32, name="ident")
+        make_identity(nc, ident[:])
+
+        pen = keep.tile([P, GROUPS * 4], F32, name="pen")
+        pen_parts = []
+        for name, vec, g0, n in (("pen_late", pen2, 0, LATE_GROUPS), ("pen_early", pen1, LATE_GROUPS, GROUPS - LATE_GROUPS)):
+            pen_raw = keep.tile([P, n, 4], BF16, name=name)
+            nc.scalar.dma_start(out=pen_raw[:], in_=vec.rearrange("(g p t) -> p g t", p=P, t=4))
+            pen_parts.append((pen_raw, g0, n))
+        for pen_raw, g0, n in pen_parts:
+            nc.scalar.activation(
+                out=pen[:, 4 * g0 : 4 * (g0 + n)], in_=pen_raw[:].rearrange("p g t -> p (g t)"), func=IDENTITY
+            )
+
+        def planes(pool, name, shape, tag, bufs):
+            codes = pool.tile(shape, U32, name=name + "_codes", tag=tag + "_codes", bufs=bufs, align_bytes=64)
+            scales = pool.tile(shape, U8, name=name + "_scales", tag=tag + "_scales", bufs=bufs, align_bytes=64)
+            return codes, scales
+
+        dy_q = [planes(keep, "dy%d" % c, [P, T], "dy%d" % c, 1) for c in range(2)]
+        df_q = [planes(keep, "df%d" % g, [P, T], "df%d" % g, 1) for g in range(GROUPS)]
+        enc_q = {(h, g): planes(keep, "enc%d_%d" % (h, g), [P, N], "enc%d_%d" % (h, g), 1) for h in range(2) for g in range(GROUPS)}
+        dec_q, acc, dx2, raws, sorted_words, banks, grouped = {}, {}, {}, {}, {}, {}, {}
+
+        def source(block):
+            kind = block[0]
+            if kind == "dy":
+                kind, jj, c = block
+                view = dy[COLS * jj : COLS * (jj + 1), :].rearrange("(a m) k -> m a k", a=2)
+                return ("dy", jj), view, c, "dy", 2
+            if kind == "dec":
+                kind, i, c = block
+                dec, gate, enc, lg = layer(i // 2)
+                rows = dec[K_PASS * lg : K_PASS * (lg + 1), :].rearrange("(m t) k -> m t k", t=4)
+                return ("dec", i), rows[:, 2 * (i % 2) : 2 * (i % 2) + 2, :], c, "dec", DEC_BUFS
+            if kind == "gate":
+                kind, g, jj = block
+                dec, gate, enc, lg = layer(g)
+                view = gate[COLS * jj : COLS * (jj + 1), K_PASS * lg : K_PASS * (lg + 1)].rearrange("(a m) k -> m a k", a=2)
+                return block, view, 0, "gate", GATE_BUFS
+            kind, h, g, pair = block
+            dec, gate, enc, lg = layer(g)
+            span = 2 if g < LATE_GROUPS else 3
+            first = lg - lg % span
+            r0 = N * h + COLS * pair
+            view = enc[r0 : r0 + COLS, K_PASS * first : K_PASS * (first + span)].rearrange("(a m) k -> m a k", a=2)
+            return ("enc", h, g - lg % span, pair), view, lg % span, "enc", ENC_BUFS
+
+        def load(block):
+            key, view, c, tag, bufs = source(block)
+            if key not in raws:
+                raws[key] = raw_pool.tile(list(view.shape), BF16, name="raw_" + tag, tag=tag, bufs=bufs)
+                nc.sync.dma_start(out=raws[key][:], in_=view)
+
+        def words_of(block):
+            key, view, c, tag, bufs = source(block)
+            return raws[key][:].bitcast(F32)[:, :, WORDS * c : WORDS * (c + 1)]
+
+        def sort(block, eng):
+            dst = work.tile([P, 2, 2, P], F32, name="sorted", tag="sorted", bufs=SORT_BUFS)
+            src = words_of(block).rearrange("m a (p u) -> m a u p", u=2)
+            if eng == "v":
+                nc.vector.tensor_copy(out=dst[:], in_=src)
+            else:
+                nc.scalar.copy(out=dst[:], in_=src)
+            sorted_words[block] = dst
+
+        def transpose(block):
+            bank = psum.tile([P, 2, COLS], F32, name="bank", tag="bank")
+            for a in range(2):
+                for u in range(2):
+                    if block in sorted_words:
+                        src = sorted_words[block][:, a, u, :]
+                    else:
+                        src = words_of(block)[:, a, u::2]
+                    nc.tensor.transpose(bank[:, u, P * a : P * (a + 1)], src, ident[:])
+            banks[block] = bank
+
+        def empty(block, eng):
+            bank = banks[block]
+            dst = work.tile([P, 4 * COLS], BF16, name="grouped", tag="grouped", bufs=GROUP_BUFS, align_bytes=64)
+            if block[0] == "gate":
+                kind, g, jj = block
+                nc.vector.tensor_tensor(
+                    out=dst[:].rearrange("p (c u e) -> p c u e", u=2, e=2),
+                    in0=acc[g][:, :, COLS * jj : COLS * (jj + 1)].rearrange("p (u e) c -> p c u e", u=2),
+                    in1=bank[:].bitcast(BF16).rearrange("p u (c e) -> p c u e", e=2),
+                    op=ALU.mult,
+                )
+            else:
+                out = dst[:].bitcast(F32).rearrange("p (c u) -> p c u", u=2)
+                src = bank[:].rearrange("p u c -> p c u")
+                if eng == "v":
+                    nc.vector.tensor_copy(out=out, in_=src)
+                else:
+                    nc.scalar.copy(out=out, in_=src)
+            grouped[block] = dst
+
+        def quantize(block):
+            kind = block[0]
+            if kind == "dy":
+                (codes, scales), c0, fmt = dy_q[block[2]], COLS * block[1], E5M2
+            elif kind == "dec":
+                if block[2] == 0:
+                    dec_q[block[1]] = planes(work, "dec", [P, 2 * COLS], "dec", 3)
+                (codes, scales), c0, fmt = dec_q[block[1]], COLS * block[2], E4M3
+            elif kind == "gate":
+                (codes, scales), c0, fmt = df_q[block[1]], COLS * block[2], E5M2
+            else:
+                (codes, scales), c0, fmt = enc_q[block[1], block[2]], COLS * block[3], E4M3
+            nc.vector.quantize_mx(
+                out=codes[:, c0 : c0 + COLS].bitcast(fmt), scales=scales[:, c0 : c0 + COLS], in_=grouped[block][:]
+            )
+
+        def multiply(mm):
+            bank = psum.tile([P, N], F32, name="bank", tag="bank")
+            if mm[0] == "df":
+                kind, i, a = mm
+                passes = [(dec_q[i], COLS * c + P * a, E4M3, dy_q[c], E5M2) for c in range(2)]
+            else:
+                kind, h, j, gs = mm
+                passes = [(df_q[g], P * j, E5M2, enc_q[h, g], E4M3) for g in gs]
+            for n, ((lc, ls), c0, lf, (rc, rs), rf) in enumerate(passes):
+                nc.tensor.matmul_mx(
+                    out=bank[:],
+                    lhsT=lc[:, c0 : c0 + P].bitcast(lf),
+                    lhsT_scale=ls[:, c0 : c0 + P],
+                    rhs=rc[:].bitcast(rf),
+                    rhs_scale=rs[:],
+                    start=(n == 0),
+                    stop=(n == len(passes) - 1),
+                )
+            return bank
+
+        def finish(mm, bank):
+            if mm[0] == "df":
+                kind, i, a = mm
+                g, t = i // 2, 2 * (i % 2) + a
+                if t == 0:
+                    acc[g] = work.tile([P, 4, T], F32, name="acc", tag="acc", bufs=ACC_BUFS)
+                nc.scalar.activation(out=acc[g][:, t, :], in_=bank[:], func=IDENTITY, bias=pen[:, 4 * g + t : 4 * g + t + 1])
+                return
+            kind, h, j, gs = mm
+            rows, cols = slice(P * j, P * (j + 1)), slice(N * h, N * (h + 1))
+            if gs[0] == 0:
+                dx2[h, j] = keep.tile([P, N], F32, name="dx2_%d_%d" % (h, j))
+                nc.scalar.copy(out=dx2[h, j][:], in_=bank[:])
+                nc.sync.dma_start(out=out_1[rows, cols], in_=dx2[h, j][:])
+            else:
+                dx1 = work.tile([P, N], F32, name="dx1", tag="dx1", bufs=4)
+                nc.vector.tensor_tensor(out=dx1[:], in0=bank[:], in1=dx2[h, j][:], op=ALU.add)
+                nc.sync.dma_start(out=out_0[rows, cols], in_=dx1[:])
+
+        items = [(s, b) for s, (blocks, mms) in enumerate(steps) for b in blocks + mms]
+        is_block = [b[0] in ("dy", "dec", "gate", "enc") for s, b in items]
+        waiting = []
+        sorted_to = 0
+        last_step = -1
+        for n, (s, item) in enumerate(items):
+            if s != last_step:
+                first = 0 if s == 0 else s + LOAD_AHEAD
+                for ahead in range(first, min(s + LOAD_AHEAD + 1, len(steps))):
+                    for b in steps[ahead][0]:
+                        load(b)
+                last_step = s
+            while sorted_to < min(n + SORT_AHEAD + 1, len(items)):
+                s2, b2 = items[sorted_to]
+                if is_block[sorted_to] and SORT(s2, b2):
+                    sort(b2, SORT(s2, b2))
+                sorted_to = sorted_to + 1
+            due = [b for at, b in waiting if at <= n]
+            waiting = [(at, b) for at, b in waiting if at > n]
+            if is_block[n]:
+                transpose(item)
+                for b in due:
+                    quantize(b)
+                empty(item, EMPTY(s, item))
+                waiting.append((n + (Q_LAG_GATE if item[0] == "gate" else Q_LAG), item))
+            else:
+                for b in due:
+                    quantize(b)
+                finish(item, multiply(item))

@@ -16,252 +16,272 @@ IDENTITY = mybir.ActivationFunctionType.Identity
 ALU = mybir.AluOpType
 
 P = 128
-K_PASS = 512
+PACK = 4
+K_PASS = P * PACK
 WORDS = K_PASS // 2
-COLS = 2 * P
+ROWS = 2 * P
 N = 512
+BANKS = 8
+LINE = 4
 LATE_GROUPS = G // K_PASS
 GROUPS = (F + G) // K_PASS
 UNITS = 2 * GROUPS
+TOKEN_TILES = T // P
 
-ENC_PER_STEP = [0, 0] + [1] * 8 + [2] * 4 + [2, 4, 3, 3, 0]
-DX_PER_STEP = [0] * 10 + [1] * 4 + [2, 2, 2, 2, 4]
 GATE_LAG = 2
-LOAD_AHEAD = 3
-SORT_AHEAD = 4
-Q_LAG = 2
-Q_LAG_GATE = 2
-DEC_BUFS, GATE_BUFS, ENC_BUFS, SORT_BUFS, GROUP_BUFS, ACC_BUFS = 5, 6, 6, 6, 5, 2
+DX_START = 2 * LATE_GROUPS + GATE_LAG
+LOAD_AHEAD = 4
+SORT_AHEAD = 10
+SORT_AHEAD_AT_START = 2
+QUANTIZE_LAG = 5
+INTERLEAVE_LAG = 8
+EARLY_SORT_END = 4
 
 
-def ORDER(decs, gates, encs):
-    return decs + gates + encs
+def plan():
+    late, early = tuple(range(LATE_GROUPS)), tuple(range(LATE_GROUPS, GROUPS))
+    halves = [(groups, h) for groups in (late, early) for h in range(D // N)]
+    enc = [("enc", h, g, r) for groups, h in halves for g in groups for r in range(2)]
+    dx = [("dx", h, j, groups) for groups, h in halves for j in range(TOKEN_TILES)]
+    steps = [[("dy", r, c) for r in range(2) for c in range(2)] + [("dec", 0, c) for c in range(2)]]
+    for i in range(UNITS + 4):
+        n_enc = 0 if i < GATE_LAG else 1 if i < DX_START else 2 if i < UNITS else 3
+        n_dx = 0 if i < DX_START else 1 if i < UNITS else 2
+        jobs = [("dec", i + 1, c) for c in range(2) if i + 1 < UNITS]
+        if 0 <= i - GATE_LAG < UNITS:
+            jobs.append(("gate",) + divmod(i - GATE_LAG, 2))
+        jobs = jobs + enc[:n_enc] + [("df", i, a) for a in range(2) if i < UNITS] + dx[:n_dx]
+        enc, dx = enc[n_enc:], dx[n_dx:]
+        steps.append(jobs)
+    steps.append(dx)
+    assert not enc
+    return steps
 
 
-def SORT(s, b):
-    return "v" if b[0] == "enc" else ""
+def length(job):
+    return len(job[3]) if job[0] == "dx" else 2
 
 
-def EMPTY(s, b):
-    return "s"
+def sorter(step, job):
+    kind = job[0]
+    if kind == "enc":
+        return "vector"
+    if kind == "dec" and (2 <= step <= EARLY_SORT_END or (step > DX_START and job[2] == 1)):
+        return "vector"
+    if kind == "gate" and step > EARLY_SORT_END and (step > DX_START or step % 2 == 1):
+        return "scalar"
+    return None
 
 
 def tile_cross_layer_transcoder_backward_s6_kernel(
     tc, dy, dec1, dec2, pen1, pen2, gate1, gate2, enc1, enc2, out_0, out_1
 ):
     nc = tc.nc
+    steps = plan()
 
     def layer(g):
-        if g < LATE_GROUPS:
-            return dec2, gate2, enc2, g
-        return dec1, gate1, enc1, g - LATE_GROUPS
-
-    late = list(range(LATE_GROUPS))
-    early = list(range(LATE_GROUPS, GROUPS))
-    enc_blocks = [("enc", h, g, pair) for gs in (late, early) for h in range(2) for pair in range(2) for g in gs]
-    dx_tiles = [("dx", h, j, gs) for gs in (late, early) for h in range(2) for j in range(T // P)]
-    steps = [([("dy", jj, c) for jj in range(2) for c in range(2)] + [("dec", 0, c) for c in range(2)], [])]
-    ne, nd = 0, 0
-    for i in range(len(ENC_PER_STEP)):
-        blocks, mms = [], []
-        decs = [("dec", i + 1, c) for c in range(2)] if i + 1 < UNITS else []
-        gates = [("gate", u // 2, u % 2) for u in range(UNITS) if min(u + GATE_LAG, UNITS) == i]
-        encs = enc_blocks[ne : ne + ENC_PER_STEP[i]]
-        ne = ne + ENC_PER_STEP[i]
-        blocks = ORDER(decs, gates, encs)
-        if i < UNITS:
-            mms = [("df", i, a) for a in range(2)]
-        mms = mms + dx_tiles[nd : nd + DX_PER_STEP[i]]
-        nd = nd + DX_PER_STEP[i]
-        steps.append((blocks, mms))
-    assert ne == len(enc_blocks) and nd == len(dx_tiles)
+        return (dec2, gate2, enc2, g) if g < LATE_GROUPS else (dec1, gate1, enc1, g - LATE_GROUPS)
 
     with ExitStack() as ctx:
         keep = ctx.enter_context(tc.tile_pool(name="keep", bufs=1))
-        raw_pool = ctx.enter_context(tc.tile_pool(name="raw", bufs=1))
-        work = ctx.enter_context(tc.tile_pool(name="work", bufs=1))
-        psum = ctx.enter_context(tc.psum_pool(name="psum", bufs=8))
+        stream = ctx.enter_context(tc.tile_pool(name="stream", bufs=1))
+        psum = ctx.enter_context(tc.psum_pool(name="psum", bufs=1))
         ctx.enter_context(tc.manual_schedule())
 
         ident = keep.tile([P, P], F32, name="ident")
         make_identity(nc, ident[:])
 
-        pen = keep.tile([P, GROUPS * 4], F32, name="pen")
-        pen_parts = []
-        for name, vec, g0, n in (("pen_late", pen2, 0, LATE_GROUPS), ("pen_early", pen1, LATE_GROUPS, GROUPS - LATE_GROUPS)):
-            pen_raw = keep.tile([P, n, 4], BF16, name=name)
-            nc.scalar.dma_start(out=pen_raw[:], in_=vec.rearrange("(g p t) -> p g t", p=P, t=4))
-            pen_parts.append((pen_raw, g0, n))
-        for pen_raw, g0, n in pen_parts:
-            nc.scalar.activation(
-                out=pen[:, 4 * g0 : 4 * (g0 + n)], in_=pen_raw[:].rearrange("p g t -> p (g t)"), func=IDENTITY
-            )
+        pen = keep.tile([P, GROUPS * PACK], F32, name="pen")
+        pen_late = keep.tile([P, LATE_GROUPS, PACK], BF16, name="pen_late")
+        pen_early = keep.tile([P, GROUPS - LATE_GROUPS, PACK], BF16, name="pen_early")
+        for pen_raw, vec in ((pen_late, pen2), (pen_early, pen1)):
+            nc.scalar.dma_start(out=pen_raw[:], in_=vec.rearrange("(g p t) -> p g t", p=P, t=PACK))
+        for pen_raw, cols in ((pen_late, slice(0, PACK * LATE_GROUPS)), (pen_early, slice(PACK * LATE_GROUPS, PACK * GROUPS))):
+            nc.scalar.activation(out=pen[:, cols], in_=pen_raw[:].rearrange("p g t -> p (g t)"), func=IDENTITY)
 
-        def planes(pool, name, shape, tag, bufs):
-            codes = pool.tile(shape, U32, name=name + "_codes", tag=tag + "_codes", bufs=bufs, align_bytes=64)
-            scales = pool.tile(shape, U8, name=name + "_scales", tag=tag + "_scales", bufs=bufs, align_bytes=64)
+        def mx_operand(pool, tag, bufs):
+            codes = pool.tile([P, N], U32, name=tag + "_codes", tag=tag + "_codes", bufs=bufs, align_bytes=64)
+            scales = pool.tile([P, N], U8, name=tag + "_scales", tag=tag + "_scales", bufs=bufs, align_bytes=64)
             return codes, scales
 
-        dy_q = [planes(keep, "dy%d" % c, [P, T], "dy%d" % c, 1) for c in range(2)]
-        df_q = [planes(keep, "df%d" % g, [P, T], "df%d" % g, 1) for g in range(GROUPS)]
-        enc_q = {(h, g): planes(keep, "enc%d_%d" % (h, g), [P, N], "enc%d_%d" % (h, g), 1) for h in range(2) for g in range(GROUPS)}
-        dec_q, acc, dx2, raws, sorted_words, banks, grouped = {}, {}, {}, {}, {}, {}, {}
+        mx = {("dy", c): mx_operand(keep, "dy%d" % c, 1) for c in range(D // K_PASS)}
+        for g in range(GROUPS):
+            mx["gate", g] = mx_operand(keep, "df%d" % g, 1)
+            for h in range(D // N):
+                mx["enc", h, g] = mx_operand(keep, "enc%d_%d" % (h, g), 1)
+        raw, by_half, pairs, grouped, sums, dx_sb = {}, {}, {}, {}, {}, {}
 
-        def source(block):
-            kind = block[0]
+        free_banks = list(range(BANKS))
+
+        def take_bank(shape):
+            number = free_banks.pop(0)
+            return number, psum.tile(shape, F32, name="bank", tag="bank%d" % number)
+
+        def source(job):
+            kind = job[0]
             if kind == "dy":
-                kind, jj, c = block
-                view = dy[COLS * jj : COLS * (jj + 1), :].rearrange("(a m) k -> m a k", a=2)
-                return ("dy", jj), view, c, "dy", 2
+                rows = dy[ROWS * job[1] : ROWS * (job[1] + 1), :]
+                return job[:2], rows.rearrange("(a m) k -> m a k", a=2), job[2], kind, 2
             if kind == "dec":
-                kind, i, c = block
-                dec, gate, enc, lg = layer(i // 2)
-                rows = dec[K_PASS * lg : K_PASS * (lg + 1), :].rearrange("(m t) k -> m t k", t=4)
-                return ("dec", i), rows[:, 2 * (i % 2) : 2 * (i % 2) + 2, :], c, "dec", DEC_BUFS
-            if kind == "gate":
-                kind, g, jj = block
+                g, s = divmod(job[1], 2)
                 dec, gate, enc, lg = layer(g)
-                view = gate[COLS * jj : COLS * (jj + 1), K_PASS * lg : K_PASS * (lg + 1)].rearrange("(a m) k -> m a k", a=2)
-                return block, view, 0, "gate", GATE_BUFS
-            kind, h, g, pair = block
+                slots = dec[K_PASS * lg : K_PASS * (lg + 1), :].rearrange("(m t) k -> m t k", t=PACK)
+                return job[:2], slots[:, 2 * s : 2 * s + 2, :], job[2], kind, LOAD_AHEAD + 2
+            if kind == "gate":
+                dec, gate, enc, lg = layer(job[1])
+                rows = gate[ROWS * job[2] : ROWS * (job[2] + 1), K_PASS * lg : K_PASS * (lg + 1)]
+                return job, rows.rearrange("(a m) k -> m a k", a=2), 0, kind, LOAD_AHEAD + 2
+            kind, h, g, r = job
             dec, gate, enc, lg = layer(g)
-            span = 2 if g < LATE_GROUPS else 3
-            first = lg - lg % span
-            r0 = N * h + COLS * pair
-            view = enc[r0 : r0 + COLS, K_PASS * first : K_PASS * (first + span)].rearrange("(a m) k -> m a k", a=2)
-            return ("enc", h, g - lg % span, pair), view, lg % span, "enc", ENC_BUFS
+            span = 2 if g < LATE_GROUPS else GROUPS - LATE_GROUPS
+            first, row0 = lg - lg % span, N * h + ROWS * r
+            rows = enc[row0 : row0 + ROWS, K_PASS * first : K_PASS * (first + span)]
+            key = (kind, h, g - lg % span, r)
+            return key, rows.rearrange("(a m) k -> m a k", a=2), lg % span, "enc%d_%d_%d" % key[1:], 1
 
-        def load(block):
-            key, view, c, tag, bufs = source(block)
-            if key not in raws:
-                raws[key] = raw_pool.tile(list(view.shape), BF16, name="raw_" + tag, tag=tag, bufs=bufs)
-                nc.sync.dma_start(out=raws[key][:], in_=view)
+        def load(job):
+            key, view, c, tag, bufs = source(job)
+            if key not in raw:
+                raw[key] = stream.tile(list(view.shape), BF16, name="raw", tag=tag, bufs=bufs)
+                nc.sync.dma_start(out=raw[key][:], in_=view)
 
-        def words_of(block):
-            key, view, c, tag, bufs = source(block)
-            return raws[key][:].bitcast(F32)[:, :, WORDS * c : WORDS * (c + 1)]
+        def words(job):
+            key, view, c, tag, bufs = source(job)
+            return raw[key][:].bitcast(F32)[:, :, WORDS * c : WORDS * (c + 1)]
 
-        def sort(block, eng):
-            dst = work.tile([P, 2, 2, P], F32, name="sorted", tag="sorted", bufs=SORT_BUFS)
-            src = words_of(block).rearrange("m a (p u) -> m a u p", u=2)
-            if eng == "v":
-                nc.vector.tensor_copy(out=dst[:], in_=src)
+        def sort(job, engine):
+            by_half[job] = stream.tile([P, 2, 2, P], F32, name="by_half", tag="by_half", bufs=SORT_AHEAD // 2 + 2)
+            src = words(job).rearrange("m a (p u) -> m a u p", u=2)
+            if engine == "vector":
+                nc.vector.tensor_copy(out=by_half[job][:], in_=src)
             else:
-                nc.scalar.copy(out=dst[:], in_=src)
-            sorted_words[block] = dst
+                nc.scalar.copy(out=by_half[job][:], in_=src)
 
-        def transpose(block):
-            bank = psum.tile([P, 2, COLS], F32, name="bank", tag="bank")
+        def transpose(job):
+            number, bank = take_bank([P, 2, ROWS])
             for a in range(2):
                 for u in range(2):
-                    if block in sorted_words:
-                        src = sorted_words[block][:, a, u, :]
-                    else:
-                        src = words_of(block)[:, a, u::2]
+                    src = by_half[job][:, a, u, :] if job in by_half else words(job)[:, a, u::2]
                     nc.tensor.transpose(bank[:, u, P * a : P * (a + 1)], src, ident[:])
-            banks[block] = bank
+            return number, bank
 
-        def empty(block, eng):
-            bank = banks[block]
-            dst = work.tile([P, 4 * COLS], BF16, name="grouped", tag="grouped", bufs=GROUP_BUFS, align_bytes=64)
-            if block[0] == "gate":
-                kind, g, jj = block
-                nc.vector.tensor_tensor(
-                    out=dst[:].rearrange("p (c u e) -> p c u e", u=2, e=2),
-                    in0=acc[g][:, :, COLS * jj : COLS * (jj + 1)].rearrange("p (u e) c -> p c u e", u=2),
-                    in1=bank[:].bitcast(BF16).rearrange("p u (c e) -> p c u e", e=2),
-                    op=ALU.mult,
-                )
-            else:
-                out = dst[:].bitcast(F32).rearrange("p (c u) -> p c u", u=2)
-                src = bank[:].rearrange("p u c -> p c u")
-                if eng == "v":
-                    nc.vector.tensor_copy(out=out, in_=src)
-                else:
-                    nc.scalar.copy(out=out, in_=src)
-            grouped[block] = dst
+        def operand(job):
+            if job[0] == "dy":
+                return ("dy", job[2]), job[1]
+            return job[:-1], job[-1]
 
-        def quantize(block):
-            kind = block[0]
-            if kind == "dy":
-                (codes, scales), c0, fmt = dy_q[block[2]], COLS * block[1], E5M2
-            elif kind == "dec":
-                if block[2] == 0:
-                    dec_q[block[1]] = planes(work, "dec", [P, 2 * COLS], "dec", 3)
-                (codes, scales), c0, fmt = dec_q[block[1]], COLS * block[2], E4M3
-            elif kind == "gate":
-                (codes, scales), c0, fmt = df_q[block[1]], COLS * block[2], E5M2
+        def interleaved(job):
+            name, half = operand(job)
+            if half == 0:
+                grouped[name] = stream.tile([P, PACK * N], BF16, name="grouped", tag="grouped", bufs=4, align_bytes=64)
+            return grouped[name][:].bitcast(F32)[:, N * half : N * (half + 1)].rearrange("p (c u) -> p c u", u=2)
+
+        def empty(job, number, bank):
+            if job[0] == "gate":
+                kind, g, r = job
+                pairs[job] = stream.tile([P, 2, 2 * ROWS], BF16, name="pairs", tag="pairs", bufs=2, align_bytes=64)
+                for u in range(2):
+                    slots = sums[g][:, 2 * u : 2 * u + 2, ROWS * r : ROWS * (r + 1)]
+                    nc.vector.tensor_tensor(
+                        out=pairs[job][:, u, :].rearrange("p (c i e) -> p c e i", i=LINE, e=2),
+                        in0=slots.rearrange("p e (c i) -> p c e i", i=LINE),
+                        in1=bank[:, u, :].bitcast(BF16).rearrange("p (c i e) -> p c e i", i=LINE, e=2),
+                        op=ALU.mult,
+                    )
             else:
-                (codes, scales), c0, fmt = enc_q[block[1], block[2]], COLS * block[3], E4M3
+                nc.scalar.copy(out=interleaved(job), in_=bank[:].rearrange("p u c -> p c u"))
+            free_banks.append(number)
+
+        def interleave_df(job):
+            nc.vector.tensor_copy(out=interleaved(job), in_=pairs[job][:].bitcast(F32).rearrange("p u c -> p c u"))
+
+        def quantize(job):
+            name, half = operand(job)
+            if job[0] == "dec" and half == 0:
+                mx[name] = mx_operand(stream, "dec", 3)
+            codes, scales = mx[name]
+            c0, c1 = (0, N) if job[0] == "gate" else (ROWS * half, ROWS * (half + 1))
             nc.vector.quantize_mx(
-                out=codes[:, c0 : c0 + COLS].bitcast(fmt), scales=scales[:, c0 : c0 + COLS], in_=grouped[block][:]
+                out=codes[:, c0:c1].bitcast(E5M2 if job[0] in ("dy", "gate") else E4M3),
+                scales=scales[:, c0:c1],
+                in_=grouped[name][:, PACK * c0 : PACK * c1],
             )
 
-        def multiply(mm):
-            bank = psum.tile([P, N], F32, name="bank", tag="bank")
-            if mm[0] == "df":
-                kind, i, a = mm
-                passes = [(dec_q[i], COLS * c + P * a, E4M3, dy_q[c], E5M2) for c in range(2)]
+        def multiply(job):
+            number, bank = take_bank([P, N])
+            if job[0] == "df":
+                kind, i, a = job
+                passes = [(mx["dec", i], ROWS * c + P * a, E4M3, mx["dy", c], E5M2) for c in range(D // K_PASS)]
             else:
-                kind, h, j, gs = mm
-                passes = [(df_q[g], P * j, E5M2, enc_q[h, g], E4M3) for g in gs]
-            for n, ((lc, ls), c0, lf, (rc, rs), rf) in enumerate(passes):
+                kind, h, j, groups = job
+                passes = [(mx["gate", g], P * j, E5M2, mx["enc", h, g], E4M3) for g in groups]
+            for n, ((l_codes, l_scales), c0, l_fmt, (r_codes, r_scales), r_fmt) in enumerate(passes):
                 nc.tensor.matmul_mx(
                     out=bank[:],
-                    lhsT=lc[:, c0 : c0 + P].bitcast(lf),
-                    lhsT_scale=ls[:, c0 : c0 + P],
-                    rhs=rc[:].bitcast(rf),
-                    rhs_scale=rs[:],
+                    lhsT=l_codes[:, c0 : c0 + P].bitcast(l_fmt),
+                    lhsT_scale=l_scales[:, c0 : c0 + P],
+                    rhs=r_codes[:].bitcast(r_fmt),
+                    rhs_scale=r_scales[:],
                     start=(n == 0),
                     stop=(n == len(passes) - 1),
                 )
-            return bank
+            return number, bank
 
-        def finish(mm, bank):
-            if mm[0] == "df":
-                kind, i, a = mm
+        def finish(job, number, bank, last):
+            if job[0] == "df":
+                kind, i, a = job
                 g, t = i // 2, 2 * (i % 2) + a
                 if t == 0:
-                    acc[g] = work.tile([P, 4, T], F32, name="acc", tag="acc", bufs=ACC_BUFS)
-                nc.scalar.activation(out=acc[g][:, t, :], in_=bank[:], func=IDENTITY, bias=pen[:, 4 * g + t : 4 * g + t + 1])
-                return
-            kind, h, j, gs = mm
-            rows, cols = slice(P * j, P * (j + 1)), slice(N * h, N * (h + 1))
-            if gs[0] == 0:
-                dx2[h, j] = keep.tile([P, N], F32, name="dx2_%d_%d" % (h, j))
-                nc.scalar.copy(out=dx2[h, j][:], in_=bank[:])
-                nc.sync.dma_start(out=out_1[rows, cols], in_=dx2[h, j][:])
+                    sums[g] = stream.tile([P, PACK, T], F32, name="sums", tag="sums", bufs=2)
+                bias = pen[:, PACK * g + t : PACK * g + t + 1]
+                nc.scalar.activation(out=sums[g][:, t, :], in_=bank[:], func=IDENTITY, bias=bias)
             else:
-                dx1 = work.tile([P, N], F32, name="dx1", tag="dx1", bufs=4)
-                nc.vector.tensor_tensor(out=dx1[:], in0=bank[:], in1=dx2[h, j][:], op=ALU.add)
-                nc.sync.dma_start(out=out_0[rows, cols], in_=dx1[:])
+                kind, h, j, groups = job
+                rows = slice(P * j, P * (j + 1))
+                if groups[0] == 0:
+                    dx_sb[h, j] = keep.tile([P, N], F32, name="dx_%d_%d" % (h, j))
+                    nc.scalar.copy(out=dx_sb[h, j][:], in_=bank[:])
+                    nc.sync.dma_start(out=out_1[rows, N * h : N * (h + 1)], in_=dx_sb[h, j][:])
+                else:
+                    width = N // 2 if last else N
+                    for c0 in range(0, N, width):
+                        part = dx_sb[h, j][:, c0 : c0 + width]
+                        nc.vector.tensor_tensor(out=part, in0=bank[:, c0 : c0 + width], in1=part, op=ALU.add)
+                        nc.sync.dma_start(out=out_0[rows, N * h + c0 : N * h + c0 + width], in_=part)
+            free_banks.append(number)
 
-        items = [(s, b) for s, (blocks, mms) in enumerate(steps) for b in blocks + mms]
-        is_block = [b[0] in ("dy", "dec", "gate", "enc") for s, b in items]
-        waiting = []
-        sorted_to = 0
-        last_step = -1
-        for n, (s, item) in enumerate(items):
-            if s != last_step:
-                first = 0 if s == 0 else s + LOAD_AHEAD
-                for ahead in range(first, min(s + LOAD_AHEAD + 1, len(steps))):
-                    for b in steps[ahead][0]:
-                        load(b)
-                last_step = s
-            while sorted_to < min(n + SORT_AHEAD + 1, len(items)):
-                s2, b2 = items[sorted_to]
-                if is_block[sorted_to] and SORT(s2, b2):
-                    sort(b2, SORT(s2, b2))
-                sorted_to = sorted_to + 1
-            due = [b for at, b in waiting if at <= n]
-            waiting = [(at, b) for at, b in waiting if at > n]
-            if is_block[n]:
-                transpose(item)
-                for b in due:
-                    quantize(b)
-                empty(item, EMPTY(s, item))
-                waiting.append((n + (Q_LAG_GATE if item[0] == "gate" else Q_LAG), item))
+        jobs = [(s, job) for s, step in enumerate(steps) for job in step]
+        starts = [sum(length(job) for s, job in jobs[:n]) for n in range(len(jobs))]
+        later = []
+        loaded, looked_at = 0, 0
+        for n, (s, job) in enumerate(jobs):
+            while loaded < min(s + LOAD_AHEAD + 1, len(steps)):
+                for ahead in steps[loaded]:
+                    if ahead[0] not in ("df", "dx"):
+                        load(ahead)
+                loaded = loaded + 1
+            now = starts[n] + length(job) - 2
+            reach = now + (SORT_AHEAD if s >= 2 else SORT_AHEAD_AT_START)
+            while looked_at < len(jobs) and starts[looked_at] <= reach:
+                engine = sorter(*jobs[looked_at])
+                if engine:
+                    sort(jobs[looked_at][1], engine)
+                looked_at = looked_at + 1
+            product = job[0] in ("df", "dx")
+            due = [(function, block) for at, function, block in later if at <= now]
+            later = [entry for entry in later if entry[0] > now]
+            if not product:
+                number, bank = transpose(job)
+            for function, block in due:
+                function(block)
+            if product:
+                number, bank = multiply(job)
+                finish(job, number, bank, n == len(jobs) - 1)
             else:
-                for b in due:
-                    quantize(b)
-                finish(item, multiply(item))
+                empty(job, number, bank)
+                if job[0] != "gate":
+                    later.append((starts[n] + QUANTIZE_LAG, quantize, job))
+                else:
+                    later.append((starts[n] + INTERLEAVE_LAG, interleave_df, job))
+                    if job[2] == 1:
+                        later.append((starts[n] + INTERLEAVE_LAG + 4, quantize, job))

from contextlib import ExitStack

import concourse.mybir as mybir
from concourse.masks import make_identity

T, D, F, G = 512, 1024, 1536, 2048
FLOPS = 4 * T * D * (F + G)

F32 = mybir.dt.float32
BF16 = mybir.dt.bfloat16
U32 = mybir.dt.uint32
U8 = mybir.dt.uint8
E4M3 = mybir.dt.float8_e4m3fn_x4
E5M2 = mybir.dt.float8_e5m2_x4
IDENTITY = mybir.ActivationFunctionType.Identity
ALU = mybir.AluOpType

P = 128
PACK = 4
K_PASS = P * PACK
WORDS = K_PASS // 2
ROWS = 2 * P
N = 512
BANKS = 8
LINE = 4
LATE_GROUPS = G // K_PASS
GROUPS = (F + G) // K_PASS
UNITS = 2 * GROUPS
TOKEN_TILES = T // P

GATE_LAG = 2
DX_START = 2 * LATE_GROUPS + GATE_LAG
LOAD_AHEAD = 4
SORT_AHEAD = 10
SORT_AHEAD_AT_START = 2
QUANTIZE_LAG = 5
INTERLEAVE_LAG = 8
EARLY_SORT_END = 4


def plan():
    late, early = tuple(range(LATE_GROUPS)), tuple(range(LATE_GROUPS, GROUPS))
    halves = [(groups, h) for groups in (late, early) for h in range(D // N)]
    enc = [("enc", h, g, r) for groups, h in halves for g in groups for r in range(2)]
    dx = [("dx", h, j, groups) for groups, h in halves for j in range(TOKEN_TILES)]
    steps = [[("dy", r, c) for r in range(2) for c in range(2)] + [("dec", 0, c) for c in range(2)]]
    for i in range(UNITS + 4):
        n_enc = 0 if i < GATE_LAG else 1 if i < DX_START else 2 if i < UNITS else 3
        n_dx = 0 if i < DX_START else 1 if i < UNITS else 2
        jobs = [("dec", i + 1, c) for c in range(2) if i + 1 < UNITS]
        if 0 <= i - GATE_LAG < UNITS:
            jobs.append(("gate",) + divmod(i - GATE_LAG, 2))
        jobs = jobs + enc[:n_enc] + [("df", i, a) for a in range(2) if i < UNITS] + dx[:n_dx]
        enc, dx = enc[n_enc:], dx[n_dx:]
        steps.append(jobs)
    steps.append(dx)
    assert not enc
    return steps


def length(job):
    return len(job[3]) if job[0] == "dx" else 2


def sorter(step, job):
    kind = job[0]
    if kind == "enc":
        return "vector"
    if kind == "dec" and (2 <= step <= EARLY_SORT_END or (step > DX_START and job[2] == 1)):
        return "vector"
    if kind == "gate" and step > EARLY_SORT_END and (step > DX_START or step % 2 == 1):
        return "scalar"
    return None


def tile_cross_layer_transcoder_backward_s6_kernel(
    tc, dy, dec1, dec2, pen1, pen2, gate1, gate2, enc1, enc2, out_0, out_1
):
    nc = tc.nc
    steps = plan()

    def layer(g):
        return (dec2, gate2, enc2, g) if g < LATE_GROUPS else (dec1, gate1, enc1, g - LATE_GROUPS)

    with ExitStack() as ctx:
        keep = ctx.enter_context(tc.tile_pool(name="keep", bufs=1))
        stream = ctx.enter_context(tc.tile_pool(name="stream", bufs=1))
        psum = ctx.enter_context(tc.psum_pool(name="psum", bufs=1))
        ctx.enter_context(tc.manual_schedule())

        ident = keep.tile([P, P], F32, name="ident")
        make_identity(nc, ident[:])

        pen = keep.tile([P, GROUPS * PACK], F32, name="pen")
        pen_late = keep.tile([P, LATE_GROUPS, PACK], BF16, name="pen_late")
        pen_early = keep.tile([P, GROUPS - LATE_GROUPS, PACK], BF16, name="pen_early")
        for pen_raw, vec in ((pen_late, pen2), (pen_early, pen1)):
            nc.scalar.dma_start(out=pen_raw[:], in_=vec.rearrange("(g p t) -> p g t", p=P, t=PACK))
        for pen_raw, cols in ((pen_late, slice(0, PACK * LATE_GROUPS)), (pen_early, slice(PACK * LATE_GROUPS, PACK * GROUPS))):
            nc.scalar.activation(out=pen[:, cols], in_=pen_raw[:].rearrange("p g t -> p (g t)"), func=IDENTITY)

        def mx_operand(pool, tag, bufs):
            codes = pool.tile([P, N], U32, name=tag + "_codes", tag=tag + "_codes", bufs=bufs, align_bytes=64)
            scales = pool.tile([P, N], U8, name=tag + "_scales", tag=tag + "_scales", bufs=bufs, align_bytes=64)
            return codes, scales

        mx = {("dy", c): mx_operand(keep, "dy%d" % c, 1) for c in range(D // K_PASS)}
        for g in range(GROUPS):
            mx["gate", g] = mx_operand(keep, "df%d" % g, 1)
            for h in range(D // N):
                mx["enc", h, g] = mx_operand(keep, "enc%d_%d" % (h, g), 1)
        raw, by_half, pairs, grouped, sums, dx_sb = {}, {}, {}, {}, {}, {}

        free_banks = list(range(BANKS))

        def take_bank(shape):
            number = free_banks.pop(0)
            return number, psum.tile(shape, F32, name="bank", tag="bank%d" % number)

        def source(job):
            kind = job[0]
            if kind == "dy":
                rows = dy[ROWS * job[1] : ROWS * (job[1] + 1), :]
                return job[:2], rows.rearrange("(a m) k -> m a k", a=2), job[2], kind, 2
            if kind == "dec":
                g, s = divmod(job[1], 2)
                dec, gate, enc, lg = layer(g)
                slots = dec[K_PASS * lg : K_PASS * (lg + 1), :].rearrange("(m t) k -> m t k", t=PACK)
                return job[:2], slots[:, 2 * s : 2 * s + 2, :], job[2], kind, LOAD_AHEAD + 2
            if kind == "gate":
                dec, gate, enc, lg = layer(job[1])
                rows = gate[ROWS * job[2] : ROWS * (job[2] + 1), K_PASS * lg : K_PASS * (lg + 1)]
                return job, rows.rearrange("(a m) k -> m a k", a=2), 0, kind, LOAD_AHEAD + 2
            kind, h, g, r = job
            dec, gate, enc, lg = layer(g)
            span = 2 if g < LATE_GROUPS else GROUPS - LATE_GROUPS
            first, row0 = lg - lg % span, N * h + ROWS * r
            rows = enc[row0 : row0 + ROWS, K_PASS * first : K_PASS * (first + span)]
            key = (kind, h, g - lg % span, r)
            return key, rows.rearrange("(a m) k -> m a k", a=2), lg % span, "enc%d_%d_%d" % key[1:], 1

        def load(job):
            key, view, c, tag, bufs = source(job)
            if key not in raw:
                raw[key] = stream.tile(list(view.shape), BF16, name="raw", tag=tag, bufs=bufs)
                nc.sync.dma_start(out=raw[key][:], in_=view)

        def words(job):
            key, view, c, tag, bufs = source(job)
            return raw[key][:].bitcast(F32)[:, :, WORDS * c : WORDS * (c + 1)]

        def sort(job, engine):
            by_half[job] = stream.tile([P, 2, 2, P], F32, name="by_half", tag="by_half", bufs=SORT_AHEAD // 2 + 2)
            src = words(job).rearrange("m a (p u) -> m a u p", u=2)
            if engine == "vector":
                nc.vector.tensor_copy(out=by_half[job][:], in_=src)
            else:
                nc.scalar.copy(out=by_half[job][:], in_=src)

        def transpose(job):
            number, bank = take_bank([P, 2, ROWS])
            for a in range(2):
                for u in range(2):
                    src = by_half[job][:, a, u, :] if job in by_half else words(job)[:, a, u::2]
                    nc.tensor.transpose(bank[:, u, P * a : P * (a + 1)], src, ident[:])
            return number, bank

        def operand(job):
            if job[0] == "dy":
                return ("dy", job[2]), job[1]
            return job[:-1], job[-1]

        def interleaved(job):
            name, half = operand(job)
            if half == 0:
                grouped[name] = stream.tile([P, PACK * N], BF16, name="grouped", tag="grouped", bufs=4, align_bytes=64)
            return grouped[name][:].bitcast(F32)[:, N * half : N * (half + 1)].rearrange("p (c u) -> p c u", u=2)

        def empty(job, number, bank):
            if job[0] == "gate":
                kind, g, r = job
                pairs[job] = stream.tile([P, 2, 2 * ROWS], BF16, name="pairs", tag="pairs", bufs=2, align_bytes=64)
                for u in range(2):
                    slots = sums[g][:, 2 * u : 2 * u + 2, ROWS * r : ROWS * (r + 1)]
                    nc.vector.tensor_tensor(
                        out=pairs[job][:, u, :].rearrange("p (c i e) -> p c e i", i=LINE, e=2),
                        in0=slots.rearrange("p e (c i) -> p c e i", i=LINE),
                        in1=bank[:, u, :].bitcast(BF16).rearrange("p (c i e) -> p c e i", i=LINE, e=2),
                        op=ALU.mult,
                    )
            else:
                nc.scalar.copy(out=interleaved(job), in_=bank[:].rearrange("p u c -> p c u"))
            free_banks.append(number)

        def interleave_df(job):
            nc.vector.tensor_copy(out=interleaved(job), in_=pairs[job][:].bitcast(F32).rearrange("p u c -> p c u"))

        def quantize(job):
            name, half = operand(job)
            if job[0] == "dec" and half == 0:
                mx[name] = mx_operand(stream, "dec", 3)
            codes, scales = mx[name]
            c0, c1 = (0, N) if job[0] == "gate" else (ROWS * half, ROWS * (half + 1))
            nc.vector.quantize_mx(
                out=codes[:, c0:c1].bitcast(E5M2 if job[0] in ("dy", "gate") else E4M3),
                scales=scales[:, c0:c1],
                in_=grouped[name][:, PACK * c0 : PACK * c1],
            )

        def multiply(job):
            number, bank = take_bank([P, N])
            if job[0] == "df":
                kind, i, a = job
                passes = [(mx["dec", i], ROWS * c + P * a, E4M3, mx["dy", c], E5M2) for c in range(D // K_PASS)]
            else:
                kind, h, j, groups = job
                passes = [(mx["gate", g], P * j, E5M2, mx["enc", h, g], E4M3) for g in groups]
            for n, ((l_codes, l_scales), c0, l_fmt, (r_codes, r_scales), r_fmt) in enumerate(passes):
                nc.tensor.matmul_mx(
                    out=bank[:],
                    lhsT=l_codes[:, c0 : c0 + P].bitcast(l_fmt),
                    lhsT_scale=l_scales[:, c0 : c0 + P],
                    rhs=r_codes[:].bitcast(r_fmt),
                    rhs_scale=r_scales[:],
                    start=(n == 0),
                    stop=(n == len(passes) - 1),
                )
            return number, bank

        def finish(job, number, bank, last):
            if job[0] == "df":
                kind, i, a = job
                g, t = i // 2, 2 * (i % 2) + a
                if t == 0:
                    sums[g] = stream.tile([P, PACK, T], F32, name="sums", tag="sums", bufs=2)
                bias = pen[:, PACK * g + t : PACK * g + t + 1]
                nc.scalar.activation(out=sums[g][:, t, :], in_=bank[:], func=IDENTITY, bias=bias)
            else:
                kind, h, j, groups = job
                rows = slice(P * j, P * (j + 1))
                if groups[0] == 0:
                    dx_sb[h, j] = keep.tile([P, N], F32, name="dx_%d_%d" % (h, j))
                    nc.scalar.copy(out=dx_sb[h, j][:], in_=bank[:])
                    nc.sync.dma_start(out=out_1[rows, N * h : N * (h + 1)], in_=dx_sb[h, j][:])
                else:
                    width = N // 2 if last else N
                    for c0 in range(0, N, width):
                        part = dx_sb[h, j][:, c0 : c0 + width]
                        nc.vector.tensor_tensor(out=part, in0=bank[:, c0 : c0 + width], in1=part, op=ALU.add)
                        nc.sync.dma_start(out=out_0[rows, N * h + c0 : N * h + c0 + width], in_=part)
            free_banks.append(number)

        jobs = [(s, job) for s, step in enumerate(steps) for job in step]
        starts = [sum(length(job) for s, job in jobs[:n]) for n in range(len(jobs))]
        later = []
        loaded, looked_at = 0, 0
        for n, (s, job) in enumerate(jobs):
            while loaded < min(s + LOAD_AHEAD + 1, len(steps)):
                for ahead in steps[loaded]:
                    if ahead[0] not in ("df", "dx"):
                        load(ahead)
                loaded = loaded + 1
            now = starts[n] + length(job) - 2
            reach = now + (SORT_AHEAD if s >= 2 else SORT_AHEAD_AT_START)
            while looked_at < len(jobs) and starts[looked_at] <= reach:
                engine = sorter(*jobs[looked_at])
                if engine:
                    sort(jobs[looked_at][1], engine)
                looked_at = looked_at + 1
            product = job[0] in ("df", "dx")
            due = [(function, block) for at, function, block in later if at <= now]
            later = [entry for entry in later if entry[0] > now]
            if not product:
                number, bank = transpose(job)
            for function, block in due:
                function(block)
            if product:
                number, bank = multiply(job)
                finish(job, number, bank, n == len(jobs) - 1)
            else:
                empty(job, number, bank)
                if job[0] != "gate":
                    later.append((starts[n] + QUANTIZE_LAG, quantize, job))
                else:
                    later.append((starts[n] + INTERLEAVE_LAG, interleave_df, job))
                    if job[2] == 1:
                        later.append((starts[n] + INTERLEAVE_LAG + 4, quantize, job))
